import numpy as np
import ml_dtypes


def mxq(x, axis, fmt="e4m3"):
    dtype, down = {"e4m3": (ml_dtypes.float8_e4m3fn, 7), "e5m2": (ml_dtypes.float8_e5m2, 14)}[fmt]
    v = np.moveaxis(np.asarray(x, np.float32).astype(ml_dtypes.bfloat16).astype(np.float64), axis, -1)
    blocks = v.reshape(v.shape[:-1] + (-1, 32))
    amax = np.abs(blocks).max(-1, keepdims=True)
    byte = np.maximum(np.where(amax > 0, np.frexp(amax)[1] - 1 + 127, 0) - down, 1)
    scale = np.exp2(byte - 127.0)
    codes = (blocks / scale).astype(np.float32).astype(dtype).astype(np.float64)
    return np.moveaxis((codes * scale).reshape(v.shape), -1, axis)


WIDE = False


def mx_kscale(k):
    if not WIDE:
        return np.ones(k)
    levels = np.array([10, -10, 5, -5, 0])
    if k % 512:
        return np.exp2(np.random.permutation(np.resize(levels, k // 32))).repeat(32)
    a = np.empty((k // 512, 16))
    for p in range(k // 512):
        a[p, :8] = np.random.permutation(np.resize(levels, 8))
        for g in range(8):
            far = levels[np.abs(levels - a[p, g]) >= 10]
            a[p, g + 8] = far[np.random.randint(len(far))]
    return np.exp2(a.ravel()).repeat(32)


def f64(x):
    return np.asarray(x).astype(np.float64)


def striped(idx):
    return np.tile(idx.reshape(-1, 16).T, (8, 1)).astype(np.uint16)


def unstriped(offs):
    return offs[:16].T.reshape(-1).astype(np.int64)


def striped8(idx):
    return np.concatenate([x.reshape(-1, 16).T for x in idx]).astype(np.uint16)


def runs(offs, k):
    lists = np.stack([offs[16 * r : 16 * r + 16].T.reshape(-1) for r in range(8)]).astype(np.int64)
    return lists[np.arange(k) % 512 // 64]


def pack_weight(w):
    k, n = w.shape
    w = f64(np.asarray(w, np.float32).astype(ml_dtypes.bfloat16)).reshape(k // 32, 32, n)
    amax = np.abs(w).max(1)
    byte = np.clip(np.where(amax > 0, np.frexp(amax)[1] - 1 + 127 - 7, 1), 1, 254)
    scaled = (w * np.exp2(127.0 - byte)[:, None, :]).reshape(k, n).astype(np.float32)
    words = np.ascontiguousarray(scaled.reshape(k // 512, 128, 4, n).transpose(0, 1, 3, 2)).astype(ml_dtypes.float8_e4m3fn).view(np.uint8)
    return words, np.ascontiguousarray(byte.astype(np.uint8).reshape(k // 512, 16, n))


def unpack_weight(words, scales):
    g, p, n, _ = words.shape
    vals = np.ascontiguousarray(words).view(ml_dtypes.float8_e4m3fn).astype(np.float64) * np.repeat(np.exp2(scales.astype(np.float64) - 127.0), 8, axis=1)[..., None]
    return vals.transpose(0, 1, 3, 2).reshape(g * 512, n)

def planes(y):
    n, m = y.shape
    v = y.astype(np.float32).astype(ml_dtypes.bfloat16).astype(np.float64).reshape(n // 32, 32, m)
    top = np.abs(v).max(1)
    byte = np.clip(np.where(top > 0, np.frexp(top)[1] - 1 + 127 - 7, 1), 1, 254)
    codes = (v * np.exp2(127.0 - byte)[:, None, :]).reshape(n, m).astype(np.float32).astype(ml_dtypes.float8_e4m3fn).view(np.uint8)
    words = codes.reshape(n // 512, 128, 4, m).transpose(0, 1, 3, 2)
    return np.ascontiguousarray(words), np.ascontiguousarray(byte.astype(np.uint8).reshape(n // 512, 16, m))


K, T, S, N, H = 512, 2048, 512, 512, 512


def setup_inputs():
    n = np.random.standard_normal
    s = mx_kscale(K)[:, None]
    u = mx_kscale(H)
    packed_xT = pack_weight(n((K, T)) * s)
    packed_w1 = pack_weight(n((K, H)) / np.sqrt(K) / s)
    packed_w2 = pack_weight(n((H, N)) / np.sqrt(H) / u[:, None])
    return {
        "x_words": packed_xT[0],
        "x_scales": packed_xT[1],
        "w1_words": packed_w1[0],
        "w1_scales": packed_w1[1],
        "gn": (np.random.uniform(0.5, 1.5, (H, 1)) * u[:, None]).astype(np.float32),
        "w2_words": packed_w2[0],
        "w2_scales": packed_w2[1],
        "offs": striped(np.random.permutation(T)[:S]),
        "n1": striped8(np.stack([np.random.permutation(S) for _ in range(8)])),
        "n2": striped8(np.stack([np.random.permutation(S) for _ in range(8)])),
        "n3": striped8(np.stack([np.random.permutation(S) for _ in range(8)])),
        "n4": striped8(np.stack([np.random.permutation(S) for _ in range(8)])),
    }


def reference(x_words, x_scales, w1_words, w1_scales, gn, w2_words, w2_scales, offs, n1, n2, n3, n4):
    xq = unpack_weight(x_words, x_scales)[:, unstriped(offs)]
    y = unpack_weight(w1_words, w1_scales).T @ xq
    z = f64(gn) * (np.minimum(np.maximum(y, y[np.arange(H)[:, None], runs(n1, H)]), y[np.arange(H)[:, None], runs(n2, H)]))
    h = unpack_weight(w2_words, w2_scales).T @ mxq(z, 0, "e4m3")
    out_0 = h * (np.tanh(y[np.arange(H)[:, None], runs(n3, H)] - (y[np.arange(H)[:, None], runs(n4, H)])))
    return (out_0,) + planes(out_0)

@@ -1,0 +1,295 @@
+from contextlib import ExitStack
+
+import concourse.mybir as mybir
+
+K, T, S, N, H = 512, 2048, 512, 512, 512
+FLOPS = 2 * K * H * S + 2 * H * N * S
+
+F32 = mybir.dt.float32
+BF16 = mybir.dt.bfloat16
+I32 = mybir.dt.int32
+U32 = mybir.dt.uint32
+U16 = mybir.dt.uint16
+U8 = mybir.dt.uint8
+FP8X4 = mybir.dt.float8_e4m3fn_x4
+ALU = mybir.AluOpType
+ACT = mybir.ActivationFunctionType
+
+P = 128
+PACK = 4
+W1_ROW = 4
+W2_ROW = 8
+CHUNKS = ((0, 256), (256, 128), (384, 128))
+
+
+def load_scale_rows(queue, tile, first_row, scales, which=range(4)):
+    rows = scales[0].bitcast(I32)
+    view = tile[:].bitcast(I32)
+    for r in which:
+        queue.dma_start(out=view[first_row + r : P : 32, :], in_=rows[r:16:4, :])
+
+
+def tile_picked_skipjointbminmx_none_po_kernel(
+    tc, x_words, x_scales, w1_words, w1_scales, gn, w2_words, w2_scales, offs, n1, n2, n3, n4, out_0, out_1, out_2
+):
+    nc = tc.nc
+    with ExitStack() as ctx:
+        lists = ctx.enter_context(tc.tile_pool(name="lists", bufs=1))
+        keep = ctx.enter_context(tc.tile_pool(name="keep", bufs=1))
+        arena = ctx.enter_context(tc.tile_pool(name="arena", bufs=1))
+        psum = ctx.enter_context(tc.psum_pool(name="psum", bufs=1))
+
+        def words_of(dram):
+            return dram[0].rearrange("p n t -> p (n t)").bitcast(I32)
+
+        offs_t = lists.tile([P, S // 16], U16, name="offs_t")
+        n1_t = lists.tile([P, S // 16], U16, name="n1_t")
+        n2_t = lists.tile([P, S // 16], U16, name="n2_t")
+        n3_t = lists.tile([P, S // 16], U16, name="n3_t")
+        n4_t = lists.tile([P, S // 16], U16, name="n4_t")
+
+        xw = keep.tile([P, T], I32, name="xw", align_bytes=64)
+        xs = keep.tile([P, T], U8, name="xs", align_bytes=64)
+        w1_raw = keep.tile([P, H], I32, name="w1_raw", align_bytes=64)
+        w2_raw = keep.tile([P, N], I32, name="w2_raw", align_bytes=64)
+        w1s_raw = keep.tile([P, H], U8, name="w1s_raw", align_bytes=64)
+        w2s_raw = keep.tile([P, N], U8, name="w2s_raw", align_bytes=64)
+        gn_t = keep.tile([P, PACK], F32, name="gn_t")
+
+        nc.gpsimd.memset(xs[:].bitcast(I32), 0)
+        nc.gpsimd.memset(w1s_raw[:].bitcast(I32), 0)
+        nc.vector.memset(w2s_raw[:].bitcast(I32), 0)
+
+        nc.sync.dma_start(offs_t[:], offs)
+        nc.sync.dma_start(out=xw[:], in_=words_of(x_words))
+        load_scale_rows(nc.scalar, xs, 0, x_scales)
+        nc.sync.dma_start(out=w1_raw[:], in_=words_of(w1_words))
+        nc.gpsimd.dma_start(out=gn_t[:], in_=gn.rearrange("(p t) o -> p (t o)", t=PACK))
+        load_scale_rows(nc.sync, w1s_raw, W1_ROW, w1_scales, range(2))
+        load_scale_rows(nc.gpsimd, w1s_raw, W1_ROW, w1_scales, range(2, 4))
+        nc.sync.dma_start(out=w2_raw[:], in_=words_of(w2_words))
+        nc.sync.dma_start(n1_t[:], n1)
+        nc.sync.dma_start(n2_t[:], n2)
+        load_scale_rows(nc.sync, w2s_raw, W2_ROW, w2_scales)
+        nc.sync.dma_start(n3_t[:], n3)
+        nc.sync.dma_start(n4_t[:], n4)
+
+        twice = keep.tile([P, PACK], F32, name="twice")
+        sign = keep.tile([P, PACK], F32, name="sign_t")
+        mag = keep.tile([P, PACK], F32, name="mag")
+        nc.gpsimd.tensor_scalar(twice[:], gn_t[:], 0.0, 2.0, ALU.is_ge, ALU.mult)
+        nc.gpsimd.tensor_scalar(sign[:], twice[:], 1.0, -1.0, ALU.mult, ALU.add)
+        nc.gpsimd.tensor_tensor(mag[:], gn_t[:], sign[:], ALU.mult)
+        warm = keep.tile([P, 1], F32, name="warm")
+        nc.scalar.activation(warm[:], gn_t[:, 0:1], ACT.Tanh)
+
+        u = [keep.tile([P, 2 * S], F32, name=f"u{t}") for t in range(PACK)]
+        for t in range(PACK):
+            nc.vector.memset(u[t][:, S:], 0.0)
+        y = [keep.tile([P, S], F32, name=f"y{t}") for t in range(PACK)]
+        ub = [keep.tile([P, S], BF16, name=f"ub{t}") for t in range(PACK)]
+
+        xg = keep.tile([P, S], U32, name="xg", align_bytes=64)
+        xsg = keep.tile([P, S], U8, name="xsg", align_bytes=64)
+        w1 = keep.tile([P, H], U32, name="w1", align_bytes=64)
+        w2 = keep.tile([P, N], U32, name="w2", align_bytes=64)
+        w1s = keep.tile([P, H], U8, name="w1s", align_bytes=64)
+
+        def deal(dst, src, engine=nc.vector):
+            engine.tensor_copy(
+                dst.rearrange("p (t m) -> p m t", t=PACK), src.rearrange("p (m t) -> p m t", t=PACK)
+            )
+
+        nc.vector.tensor_copy(xsg[:], xs[:].indirect(offs_t[:]))
+        deal(w1s[:], w1s_raw[:])
+        half = S // 2
+        nc.vector.tensor_copy(xg[:, :half], xw[:].bitcast(U32).indirect(offs_t[:, : half // 16]))
+        deal(w1[:], w1_raw[:].bitcast(U32))
+        nc.vector.tensor_copy(xg[:, half:], xw[:].bitcast(U32).indirect(offs_t[:, half // 16 :]))
+        deal(w2[:], w2_raw[:].bitcast(U32))
+
+        y_ps = [psum.tile([P, S], F32, name=f"y_ps{t}") for t in range(PACK)]
+
+        def first_product(t, a, b):
+            m = slice(t * P, (t + 1) * P)
+            nc.tensor.matmul_mx(
+                out=y_ps[t][:, a:b], lhsT=w1[:, m].bitcast(FP8X4), lhsT_scale=w1s[W1_ROW:P, m],
+                rhs=xg[:, a:b].bitcast(FP8X4), rhs_scale=xsg[:, a:b], start=True, stop=True,
+            )
+            if t > 0:
+                nc.scalar.activation(ub[t][:], y_ps[t][:], ACT.Copy, scale=mag[:, t : t + 1])
+            nc.scalar.activation(u[t][:, a:b], y_ps[t][:, a:b], ACT.Copy, scale=mag[:, t : t + 1])
+
+        first_product(0, 0, half)
+        first_product(0, half, S)
+        nc.scalar.activation(ub[0][:], y_ps[0][:], ACT.Copy, scale=mag[:, 0:1])
+        KB = 1024
+        place = {"zs": 0, "d0": 4 * KB, "th0": 8 * KB, "d1": 12 * KB}
+        for t in range(PACK):
+            place["g1", t] = (14 + t) * KB
+            place["g2", t] = (18 + t) * KB
+            place["mx", t] = (22 + t) * KB
+        g4_place = {
+            (0, 0): place["g1", 3], (0, 1): place["g2", 2], (0, 2): place["mx", 3], (0, 3): place["g2", 3],
+            (1, 0): place["zs"], (1, 1): place["zs"] + KB, (1, 2): place["d0"], (1, 3): place["d0"] + KB,
+            (2, 0): place["th0"], (2, 1): place["th0"] + KB, (2, 2): place["d1"], (2, 3): place["d1"] + KB,
+        }
+        zs = arena.tile([P, PACK, S], BF16, name="zs", offset=place["zs"])
+        g1, g2, mx = {}, {}, {}
+        mn_last = keep.tile([P, S], BF16, name="mn_last")
+
+        def pick1(t):
+            g1[t] = arena.tile([P, S], BF16, name=f"g1_{t}", offset=place["g1", t])
+            nc.vector.tensor_copy(g1[t][:], u[t][:].indirect(n1_t[:]))
+
+        def pick2(t):
+            g2[t] = arena.tile([P, S], BF16, name=f"g2_{t}", offset=place["g2", t])
+            nc.vector.tensor_copy(g2[t][:], u[t][:].indirect(n2_t[:]))
+
+        def larger(t):
+            mx[t] = arena.tile([P, S], BF16, name=f"mx_{t}", offset=place["mx", t])
+            nc.vector.tensor_tensor(mx[t][:], ub[t][:], g1[t][:], ALU.max)
+
+        def smaller(t):
+            mn = u[t + 1][:, S:].bitcast(BF16)[:, :S] if t + 1 < PACK else mn_last[:]
+            nc.vector.tensor_tensor(mn, mx[t][:], g2[t][:], ALU.min)
+            nc.scalar.activation(zs[:, t, :], mn, ACT.Copy, scale=sign[:, t : t + 1])
+
+        for t in range(PACK):
+            if t + 1 < PACK:
+                first_product(t + 1, 0, S)
+            pick1(t)
+            pick2(t)
+            larger(t)
+            nc.scalar.copy(y[t][:], y_ps[t][:])
+            if t > 0:
+                smaller(t - 1)
+
+        w2s = arena.tile([P, N], U8, name="w2s", align_bytes=64, offset=place["g1", 0])
+        deal(w2s[:], w2s_raw[:])
+        d, g4, th, o, h_ps = {}, {}, {}, {}, {}
+        d[0] = arena.tile([P, PACK, 256], F32, name="d0", offset=place["d0"])
+        d[1] = arena.tile([P, PACK, 128], F32, name="d1", offset=place["d1"])
+        d[2] = keep.tile([P, PACK, 128], F32, name="d2")
+        th[0] = arena.tile([P, PACK, 256], F32, name="th0", offset=place["th0"])
+        th[1] = keep.tile([P, PACK, 128], F32, name="th1")
+        th[2] = keep.tile([P, PACK, 128], F32, name="th2")
+        for c, (a, w) in enumerate(CHUNKS):
+            o[c] = keep.tile([P, PACK, w], F32, name=f"o{c}")
+
+        def pick4(c, t):
+            a, w = CHUNKS[c]
+            g4[c, t] = arena.tile([P, w], F32, name=f"g4_{c}_{t}", offset=g4_place[c, t])
+            nc.vector.tensor_copy(g4[c, t][:], y[t][:].indirect(n4_t[:, a // 16 : (a + w) // 16]))
+
+        def pick3(c, t):
+            a, w = CHUNKS[c]
+            nc.vector.tensor_tensor(
+                d[c][:, t, :], y[t][:].indirect(n3_t[:, a // 16 : (a + w) // 16]), g4[c, t][:], ALU.subtract
+            )
+            nc.scalar.activation(th[c][:, t, :], d[c][:, t, :], ACT.Tanh)
+
+        zq = keep.tile([P, S], U32, name="zq", align_bytes=64)
+        zqs = keep.tile([P, S], U8, name="zqs", align_bytes=64)
+        zi = keep.tile([P, S, PACK], BF16, name="zi", align_bytes=64)
+
+        def weave_z():
+            nc.scalar.copy(
+                zi[:].rearrange("p (c i) t -> p c t i", i=4),
+                zs[:].rearrange("p t (c i) -> p c t i", i=4),
+            )
+
+        def quantize_z():
+            nc.vector.quantize_mx(out=zq[:].bitcast(FP8X4), scales=zqs[:], in_=zi[:].rearrange("p c t -> p (c t)"))
+
+        def second_product(c):
+            a, w = CHUNKS[c]
+            per_bank = S // w
+            for b in range(PACK // per_bank):
+                h_ps[c, b] = psum.tile([P, per_bank, w], F32, name=f"h_ps{c}_{b}")
+                for i in range(per_bank):
+                    t = b * per_bank + i
+                    m = slice(t * P, (t + 1) * P)
+                    nc.tensor.matmul_mx(
+                        out=h_ps[c, b][:, i, :], lhsT=w2[:, m].bitcast(FP8X4), lhsT_scale=w2s[W2_ROW:P, m],
+                        rhs=zq[:, a : a + w].bitcast(FP8X4), rhs_scale=zqs[:, a : a + w], start=True, stop=True,
+                    )
+
+        oq = keep.tile([P, S], U32, name="oq", align_bytes=64)
+        oqs = keep.tile([P, S], U8, name="oqs", align_bytes=64)
+        oi = {}
+        out_rows = out_0.rearrange("(p t) j -> p t j", t=PACK)
+        out_words = words_of(out_1)
+
+        def gate(c, t0, t1):
+            a, w = CHUNKS[c]
+            per_bank = S // w
+            b = t0 // per_bank
+            nc.vector.tensor_tensor(
+                o[c][:, t0:t1, :], h_ps[c, b][:, t0 - b * per_bank : t1 - b * per_bank, :], th[c][:, t0:t1, :], ALU.mult
+            )
+
+        def weave_out(c):
+            a, w = CHUNKS[c]
+            nc.sync.dma_start(out=out_rows[:, :, a : a + w], in_=o[c][:])
+            oi[c] = keep.tile([P, w, PACK], BF16, name=f"oi{c}", align_bytes=64)
+            nc.scalar.copy(
+                oi[c][:].rearrange("p (c i) t -> p c t i", i=4),
+                o[c][:].rearrange("p t (c i) -> p c t i", i=4),
+            )
+
+        def quantize_out(c):
+            a, w = CHUNKS[c]
+            nc.vector.quantize_mx(
+                out=oq[:, a : a + w].bitcast(FP8X4), scales=oqs[:, a : a + w],
+                in_=oi[c][:].rearrange("p c t -> p (c t)"),
+            )
+            nc.sync.dma_start(out=out_words[:, a : a + w], in_=oq[:, a : a + w].bitcast(I32))
+
+        pick4(0, 0)
+        smaller(PACK - 1)
+        weave_z()
+        pick4(0, 1)
+        pick3(0, 0)
+        pick4(0, 2)
+        pick3(0, 1)
+        pick4(0, 3)
+        pick3(0, 2)
+        pick3(0, 3)
+        quantize_z()
+        second_product(0)
+        second_product(1)
+        second_product(2)
+        pick4(1, 0)
+        pick4(1, 1)
+        pick3(1, 0)
+        pick3(1, 1)
+        gate(0, 0, 2)
+        gate(0, 2, 4)
+        weave_out(0)
+        pick4(1, 2)
+        pick4(1, 3)
+        pick3(1, 2)
+        pick3(1, 3)
+        pick4(2, 0)
+        pick4(2, 1)
+        pick3(2, 0)
+        pick3(2, 1)
+        quantize_out(0)
+        gate(1, 0, 4)
+        weave_out(1)
+        pick4(2, 2)
+        pick4(2, 3)
+        pick3(2, 2)
+        pick3(2, 3)
+        quantize_out(1)
+        gate(2, 0, 2)
+        gate(2, 2, 4)
+        weave_out(2)
+        quantize_out(2)
+
+        scale_rows = out_2[0].bitcast(I32)
+        live = oqs[:].bitcast(I32)
+        for q in range(4):
+            queue = nc.sync if q % 2 == 0 else nc.scalar
+            queue.dma_start(out=scale_rows[4 * q : 4 * q + 4, :], in_=live[32 * q : 32 * q + 4, :])

@@ -19,7 +19,7 @@ P = 128
 PACK = 4
 W1_ROW = 4
 W2_ROW = 8
-CHUNKS = ((0, 256), (256, 128), (384, 128))
+CHUNKS = ((0, 256), (256, 256))
 
 
 def load_scale_rows(queue, tile, first_row, scales, which=range(4)):
@@ -58,21 +58,20 @@ def tile_picked_skipjointbminmx_none_po_kernel(
 
         nc.gpsimd.memset(xs[:].bitcast(I32), 0)
         nc.gpsimd.memset(w1s_raw[:].bitcast(I32), 0)
-        nc.vector.memset(w2s_raw[:].bitcast(I32), 0)
+        nc.gpsimd.memset(w2s_raw[:].bitcast(I32), 0)
 
         nc.sync.dma_start(offs_t[:], offs)
-        nc.sync.dma_start(out=xw[:], in_=words_of(x_words))
-        load_scale_rows(nc.scalar, xs, 0, x_scales)
-        nc.sync.dma_start(out=w1_raw[:], in_=words_of(w1_words))
-        nc.gpsimd.dma_start(out=gn_t[:], in_=gn.rearrange("(p t) o -> p (t o)", t=PACK))
-        load_scale_rows(nc.sync, w1s_raw, W1_ROW, w1_scales, range(2))
-        load_scale_rows(nc.gpsimd, w1s_raw, W1_ROW, w1_scales, range(2, 4))
-        nc.sync.dma_start(out=w2_raw[:], in_=words_of(w2_words))
         nc.sync.dma_start(n1_t[:], n1)
+        load_scale_rows(nc.sync, xs, 0, x_scales)
+        nc.sync.dma_start(out=w1_raw[:], in_=words_of(w1_words))
+        nc.sync.dma_start(out=xw[:], in_=words_of(x_words))
+        nc.gpsimd.dma_start(out=gn_t[:], in_=gn.rearrange("(p t) o -> p (t o)", t=PACK))
+        load_scale_rows(nc.sync, w1s_raw, W1_ROW, w1_scales)
         nc.sync.dma_start(n2_t[:], n2)
+        nc.sync.dma_start(n4_t[:], n4)
+        nc.sync.dma_start(out=w2_raw[:], in_=words_of(w2_words))
         load_scale_rows(nc.sync, w2s_raw, W2_ROW, w2_scales)
         nc.sync.dma_start(n3_t[:], n3)
-        nc.sync.dma_start(n4_t[:], n4)
 
         twice = keep.tile([P, PACK], F32, name="twice")
         sign = keep.tile([P, PACK], F32, name="sign_t")
@@ -84,9 +83,7 @@ def tile_picked_skipjointbminmx_none_po_kernel(
         nc.scalar.activation(warm[:], gn_t[:, 0:1], ACT.Tanh)
 
         u = [keep.tile([P, 2 * S], F32, name=f"u{t}") for t in range(PACK)]
-        for t in range(PACK):
-            nc.vector.memset(u[t][:, S:], 0.0)
-        y = [keep.tile([P, S], F32, name=f"y{t}") for t in range(PACK)]
+        y = [keep.tile([P, 2 * S], F32, name=f"y{t}") for t in range(PACK)]
         ub = [keep.tile([P, S], BF16, name=f"ub{t}") for t in range(PACK)]
 
         xg = keep.tile([P, S], U32, name="xg", align_bytes=64)
@@ -95,18 +92,18 @@ def tile_picked_skipjointbminmx_none_po_kernel(
         w2 = keep.tile([P, N], U32, name="w2", align_bytes=64)
         w1s = keep.tile([P, H], U8, name="w1s", align_bytes=64)
 
-        def deal(dst, src, engine=nc.vector):
-            engine.tensor_copy(
-                dst.rearrange("p (t m) -> p m t", t=PACK), src.rearrange("p (m t) -> p m t", t=PACK)
+        def deal(dst, src, line):
+            nc.vector.tensor_copy(
+                dst.rearrange("p (t c i) -> p c t i", t=PACK, i=line), src.rearrange("p (c i t) -> p c t i", t=PACK, i=line)
             )
 
         nc.vector.tensor_copy(xsg[:], xs[:].indirect(offs_t[:]))
-        deal(w1s[:], w1s_raw[:])
+        deal(w1[:], w1_raw[:].bitcast(U32), 4)
         half = S // 2
         nc.vector.tensor_copy(xg[:, :half], xw[:].bitcast(U32).indirect(offs_t[:, : half // 16]))
-        deal(w1[:], w1_raw[:].bitcast(U32))
+        deal(w1s[:], w1s_raw[:], 16)
         nc.vector.tensor_copy(xg[:, half:], xw[:].bitcast(U32).indirect(offs_t[:, half // 16 :]))
-        deal(w2[:], w2_raw[:].bitcast(U32))
+        deal(w2[:], w2_raw[:].bitcast(U32), 4)
 
         y_ps = [psum.tile([P, S], F32, name=f"y_ps{t}") for t in range(PACK)]
 
@@ -124,16 +121,15 @@ def tile_picked_skipjointbminmx_none_po_kernel(
         first_product(0, half, S)
         nc.scalar.activation(ub[0][:], y_ps[0][:], ACT.Copy, scale=mag[:, 0:1])
         KB = 1024
-        place = {"zs": 0, "d0": 4 * KB, "th0": 8 * KB, "d1": 12 * KB}
+        place = {"zs": 0, "d0": 0}
+        for t in range(PACK - 1):
+            place["g1", t] = (4 + t) * KB
+            place["g2", t] = (7 + t) * KB
         for t in range(PACK):
-            place["g1", t] = (14 + t) * KB
-            place["g2", t] = (18 + t) * KB
-            place["mx", t] = (22 + t) * KB
-        g4_place = {
-            (0, 0): place["g1", 3], (0, 1): place["g2", 2], (0, 2): place["mx", 3], (0, 3): place["g2", 3],
-            (1, 0): place["zs"], (1, 1): place["zs"] + KB, (1, 2): place["d0"], (1, 3): place["d0"] + KB,
-            (2, 0): place["th0"], (2, 1): place["th0"] + KB, (2, 2): place["d1"], (2, 3): place["d1"] + KB,
-        }
+            place["mx", t] = (10 + t) * KB
+        place["g1", 3] = 16 * KB
+        place["g2", 3] = 21 * KB
+        g4_place = [place["g1", 3] - 3 * KB // 2, place["g1", 3] + KB // 2, place["g2", 3] - 3 * KB // 2, place["g2", 3] + KB // 2]
         zs = arena.tile([P, PACK, S], BF16, name="zs", offset=place["zs"])
         g1, g2, mx = {}, {}, {}
         mn_last = keep.tile([P, S], BF16, name="mn_last")
@@ -161,33 +157,31 @@ def tile_picked_skipjointbminmx_none_po_kernel(
             pick1(t)
             pick2(t)
             larger(t)
-            nc.scalar.copy(y[t][:], y_ps[t][:])
+            nc.scalar.copy(y[t][:, :S], y_ps[t][:])
             if t > 0:
                 smaller(t - 1)
 
         w2s = arena.tile([P, N], U8, name="w2s", align_bytes=64, offset=place["g1", 0])
-        deal(w2s[:], w2s_raw[:])
+        deal(w2s[:], w2s_raw[:], 16)
         d, g4, th, o, h_ps = {}, {}, {}, {}, {}
-        d[0] = arena.tile([P, PACK, 256], F32, name="d0", offset=place["d0"])
-        d[1] = arena.tile([P, PACK, 128], F32, name="d1", offset=place["d1"])
-        d[2] = keep.tile([P, PACK, 128], F32, name="d2")
-        th[0] = arena.tile([P, PACK, 256], F32, name="th0", offset=place["th0"])
-        th[1] = keep.tile([P, PACK, 128], F32, name="th1")
-        th[2] = keep.tile([P, PACK, 128], F32, name="th2")
+        d[0] = arena.tile([P, PACK, 256], F32, name="d0", offset=place["zs"] + 0)
+        d_late = arena.tile([P, PACK - 1, 256], F32, name="d_late", offset=place["d0"])
+        d_first = arena.tile([P, 256], F32, name="d_first", offset=place["mx", 3])
         for c, (a, w) in enumerate(CHUNKS):
+            th[c] = keep.tile([P, PACK, w], F32, name=f"th{c}")
             o[c] = keep.tile([P, PACK, w], F32, name=f"o{c}")
 
-        def pick4(c, t):
-            a, w = CHUNKS[c]
-            g4[c, t] = arena.tile([P, w], F32, name=f"g4_{c}_{t}", offset=g4_place[c, t])
-            nc.vector.tensor_copy(g4[c, t][:], y[t][:].indirect(n4_t[:, a // 16 : (a + w) // 16]))
+        def pick4(t):
+            g4[t] = arena.tile([P, S], F32, name=f"g4_{t}", offset=g4_place[t])
+            nc.vector.tensor_copy(g4[t][:], y[t][:].indirect(n4_t[:]))
 
         def pick3(c, t):
             a, w = CHUNKS[c]
+            diff = d[0][:, t, :] if c == 0 else (d_first[:] if t == 0 else d_late[:, t - 1, :])
             nc.vector.tensor_tensor(
-                d[c][:, t, :], y[t][:].indirect(n3_t[:, a // 16 : (a + w) // 16]), g4[c, t][:], ALU.subtract
+                diff, y[t][:].indirect(n3_t[:, a // 16 : (a + w) // 16]), g4[t][:, a : a + w], ALU.subtract
             )
-            nc.scalar.activation(th[c][:, t, :], d[c][:, t, :], ACT.Tanh)
+            nc.scalar.activation(th[c][:, t, :], diff, ACT.Tanh)
 
         zq = keep.tile([P, S], U32, name="zq", align_bytes=64)
         zqs = keep.tile([P, S], U8, name="zqs", align_bytes=64)
@@ -229,14 +223,16 @@ def tile_picked_skipjointbminmx_none_po_kernel(
                 o[c][:, t0:t1, :], h_ps[c, b][:, t0 - b * per_bank : t1 - b * per_bank, :], th[c][:, t0:t1, :], ALU.mult
             )
 
-        def weave_out(c):
+        def weave_out(c, engines):
             a, w = CHUNKS[c]
             nc.sync.dma_start(out=out_rows[:, :, a : a + w], in_=o[c][:])
             oi[c] = keep.tile([P, w, PACK], BF16, name=f"oi{c}", align_bytes=64)
-            nc.scalar.copy(
-                oi[c][:].rearrange("p (c i) t -> p c t i", i=4),
-                o[c][:].rearrange("p t (c i) -> p c t i", i=4),
-            )
+            share = w // len(engines)
+            for k, copy in enumerate(engines):
+                copy(
+                    oi[c][:, k * share : (k + 1) * share, :].rearrange("p (c i) t -> p c t i", i=4),
+                    o[c][:, :, k * share : (k + 1) * share].rearrange("p t (c i) -> p c t i", i=4),
+                )
 
         def quantize_out(c):
             a, w = CHUNKS[c]
@@ -246,47 +242,27 @@ def tile_picked_skipjointbminmx_none_po_kernel(
             )
             nc.sync.dma_start(out=out_words[:, a : a + w], in_=oq[:, a : a + w].bitcast(I32))
 
-        pick4(0, 0)
+        pick4(0)
         smaller(PACK - 1)
         weave_z()
-        pick4(0, 1)
-        pick3(0, 0)
-        pick4(0, 2)
-        pick3(0, 1)
-        pick4(0, 3)
-        pick3(0, 2)
-        pick3(0, 3)
+        for t in range(1, PACK):
+            pick4(t)
         quantize_z()
         second_product(0)
         second_product(1)
-        second_product(2)
-        pick4(1, 0)
-        pick4(1, 1)
+        for t in range(PACK):
+            pick3(0, t)
         pick3(1, 0)
-        pick3(1, 1)
         gate(0, 0, 2)
         gate(0, 2, 4)
-        weave_out(0)
-        pick4(1, 2)
-        pick4(1, 3)
-        pick3(1, 2)
-        pick3(1, 3)
-        pick4(2, 0)
-        pick4(2, 1)
-        pick3(2, 0)
-        pick3(2, 1)
+        weave_out(0, [nc.scalar.copy])
+        for t in range(1, PACK):
+            pick3(1, t)
         quantize_out(0)
-        gate(1, 0, 4)
-        weave_out(1)
-        pick4(2, 2)
-        pick4(2, 3)
-        pick3(2, 2)
-        pick3(2, 3)
+        gate(1, 0, 2)
+        gate(1, 2, 4)
+        weave_out(1, [nc.scalar.copy, nc.vector.tensor_copy])
         quantize_out(1)
-        gate(2, 0, 2)
-        gate(2, 2, 4)
-        weave_out(2)
-        quantize_out(2)
 
         scale_rows = out_2[0].bitcast(I32)
         live = oqs[:].bitcast(I32)

@@ -37,6 +37,7 @@ def tile_picked_skipjointbminmx_none_po_kernel(
         lists = ctx.enter_context(tc.tile_pool(name="lists", bufs=1))
         keep = ctx.enter_context(tc.tile_pool(name="keep", bufs=1))
         arena = ctx.enter_context(tc.tile_pool(name="arena", bufs=1))
+        head = ctx.enter_context(tc.tile_pool(name="head", bufs=1))
         psum = ctx.enter_context(tc.psum_pool(name="psum", bufs=1))
 
         def words_of(dram):
@@ -48,7 +49,7 @@ def tile_picked_skipjointbminmx_none_po_kernel(
         n3_t = lists.tile([P, S // 16], U16, name="n3_t")
         n4_t = lists.tile([P, S // 16], U16, name="n4_t")
 
-        xw = keep.tile([P, T], I32, name="xw", align_bytes=64)
+        xw = head.tile([P, T], I32, name="xw", align_bytes=64, offset=0)
         xs = keep.tile([P, T], U8, name="xs", align_bytes=64)
         w1_raw = keep.tile([P, H], I32, name="w1_raw", align_bytes=64)
         w2_raw = keep.tile([P, N], I32, name="w2_raw", align_bytes=64)
@@ -63,13 +64,13 @@ def tile_picked_skipjointbminmx_none_po_kernel(
         nc.sync.dma_start(offs_t[:], offs)
         nc.sync.dma_start(n1_t[:], n1)
         load_scale_rows(nc.sync, xs, 0, x_scales)
-        nc.sync.dma_start(out=w1_raw[:], in_=words_of(w1_words))
         nc.sync.dma_start(out=xw[:], in_=words_of(x_words))
+        nc.sync.dma_start(out=w1_raw[:], in_=words_of(w1_words))
         nc.gpsimd.dma_start(out=gn_t[:], in_=gn.rearrange("(p t) o -> p (t o)", t=PACK))
         load_scale_rows(nc.sync, w1s_raw, W1_ROW, w1_scales)
+        nc.sync.dma_start(out=w2_raw[:], in_=words_of(w2_words))
         nc.sync.dma_start(n2_t[:], n2)
         nc.sync.dma_start(n4_t[:], n4)
-        nc.sync.dma_start(out=w2_raw[:], in_=words_of(w2_words))
         load_scale_rows(nc.sync, w2s_raw, W2_ROW, w2_scales)
         nc.sync.dma_start(n3_t[:], n3)
 
@@ -84,91 +85,94 @@ def tile_picked_skipjointbminmx_none_po_kernel(
 
         u = [keep.tile([P, 2 * S], F32, name=f"u{t}") for t in range(PACK)]
         y = [keep.tile([P, 2 * S], F32, name=f"y{t}") for t in range(PACK)]
-        ub = [keep.tile([P, S], BF16, name=f"ub{t}") for t in range(PACK)]
+        ub = [keep.tile([P, 2, S], BF16, name=f"ub{k}") for k in range(2)]
 
         xg = keep.tile([P, S], U32, name="xg", align_bytes=64)
         xsg = keep.tile([P, S], U8, name="xsg", align_bytes=64)
-        w1 = keep.tile([P, H], U32, name="w1", align_bytes=64)
-        w2 = keep.tile([P, N], U32, name="w2", align_bytes=64)
-        w1s = keep.tile([P, H], U8, name="w1s", align_bytes=64)
+        w1 = head.tile([P, H], U32, name="w1", align_bytes=64, offset=0)
+        w2 = head.tile([P, N], U32, name="w2", align_bytes=64, offset=2048)
+        w1s = head.tile([P, H], U8, name="w1s", align_bytes=64, offset=4096)
 
-        def deal(dst, src, line):
+        def deal(dst, src, line, t0=0, t1=PACK):
             nc.vector.tensor_copy(
-                dst.rearrange("p (t c i) -> p c t i", t=PACK, i=line), src.rearrange("p (c i t) -> p c t i", t=PACK, i=line)
+                dst.rearrange("p (t c i) -> p c t i", t=PACK, i=line)[:, :, t0:t1, :],
+                src.rearrange("p (c i t) -> p c t i", t=PACK, i=line)[:, :, t0:t1, :],
             )
 
         nc.vector.tensor_copy(xsg[:], xs[:].indirect(offs_t[:]))
-        deal(w1[:], w1_raw[:].bitcast(U32), 4)
-        half = S // 2
-        nc.vector.tensor_copy(xg[:, :half], xw[:].bitcast(U32).indirect(offs_t[:, : half // 16]))
-        deal(w1s[:], w1s_raw[:], 16)
-        nc.vector.tensor_copy(xg[:, half:], xw[:].bitcast(U32).indirect(offs_t[:, half // 16 :]))
+        nc.vector.tensor_copy(xg[:], xw[:].bitcast(U32).indirect(offs_t[:]))
+        deal(w1[:], w1_raw[:].bitcast(U32), 4, 0, 1)
+        deal(w1s[:], w1s_raw[:], 16, 0, 1)
+        deal(w1[:], w1_raw[:].bitcast(U32), 4, 1, PACK)
+        deal(w1s[:], w1s_raw[:], 16, 1, PACK)
         deal(w2[:], w2_raw[:].bitcast(U32), 4)
 
         y_ps = [psum.tile([P, S], F32, name=f"y_ps{t}") for t in range(PACK)]
+        half = S // 2
+        y_late = psum.tile([P, half], F32, name="y_late", tag="h_ps1_1")
 
-        def first_product(t, a, b):
+        def first_product(t, bank, a, b):
             m = slice(t * P, (t + 1) * P)
             nc.tensor.matmul_mx(
-                out=y_ps[t][:, a:b], lhsT=w1[:, m].bitcast(FP8X4), lhsT_scale=w1s[W1_ROW:P, m],
+                out=bank, lhsT=w1[:, m].bitcast(FP8X4), lhsT_scale=w1s[W1_ROW:P, m],
                 rhs=xg[:, a:b].bitcast(FP8X4), rhs_scale=xsg[:, a:b], start=True, stop=True,
             )
-            if t > 0:
-                nc.scalar.activation(ub[t][:], y_ps[t][:], ACT.Copy, scale=mag[:, t : t + 1])
-            nc.scalar.activation(u[t][:, a:b], y_ps[t][:, a:b], ACT.Copy, scale=mag[:, t : t + 1])
 
-        first_product(0, 0, half)
-        first_product(0, half, S)
-        nc.scalar.activation(ub[0][:], y_ps[0][:], ACT.Copy, scale=mag[:, 0:1])
+        def scaled(dst, bank, t):
+            nc.scalar.activation(dst, bank, ACT.Copy, scale=mag[:, t : t + 1])
+
+        first_product(0, y_ps[0][:, :half], 0, half)
+        first_product(0, y_late[:], half, S)
+        scaled(u[0][:, :half], y_ps[0][:, :half], 0)
+        nc.vector.tensor_scalar(u[0][:, half:S], y_late[:], mag[:, 0:1], None, ALU.mult)
+        nc.scalar.copy(ub[0][:, 0, :], u[0][:, :S])
+        for t in range(1, PACK):
+            first_product(t, y_ps[t][:], 0, S)
+            scaled(ub[t // 2][:, t % 2, :], y_ps[t][:], t)
+            scaled(u[t][:, :S], y_ps[t][:], t)
+        nc.scalar.copy(y[0][:, :half], y_ps[0][:, :half])
+        nc.scalar.copy(y[0][:, half:S], y_late[:])
+        for t in range(1, PACK):
+            nc.scalar.copy(y[t][:, :S], y_ps[t][:])
+
         KB = 1024
-        place = {"zs": 0, "d0": 0}
-        for t in range(PACK - 1):
-            place["g1", t] = (4 + t) * KB
-            place["g2", t] = (7 + t) * KB
-        for t in range(PACK):
-            place["mx", t] = (10 + t) * KB
-        place["g1", 3] = 16 * KB
-        place["g2", 3] = 21 * KB
-        g4_place = [place["g1", 3] - 3 * KB // 2, place["g1", 3] + KB // 2, place["g2", 3] - 3 * KB // 2, place["g2", 3] + KB // 2]
+        place = {"zs": 0, "d0": 0, ("g1", 0): 4 * KB, ("g2", 0): 6 * KB, ("mx", 0): 8 * KB, ("mx", 1): 10 * KB}
+        place["g1", 1] = 14 * KB
+        place["g2", 1] = 20 * KB
+        g4_place = [place["g1", 1] - KB, place["g1", 1] + KB, place["g2", 1] - KB, place["g2", 1] + KB]
         zs = arena.tile([P, PACK, S], BF16, name="zs", offset=place["zs"])
         g1, g2, mx = {}, {}, {}
-        mn_last = keep.tile([P, S], BF16, name="mn_last")
+        mn_last = arena.tile([P, 2, S], BF16, name="mn_last", offset=26 * KB)
 
-        def pick1(t):
-            g1[t] = arena.tile([P, S], BF16, name=f"g1_{t}", offset=place["g1", t])
-            nc.vector.tensor_copy(g1[t][:], u[t][:].indirect(n1_t[:]))
+        def larger(k):
+            mx[k] = arena.tile([P, 2, S], BF16, name=f"mx_{k}", offset=place["mx", k])
+            nc.vector.tensor_tensor(mx[k][:], ub[k][:], g1[k][:], ALU.max)
 
-        def pick2(t):
-            g2[t] = arena.tile([P, S], BF16, name=f"g2_{t}", offset=place["g2", t])
-            nc.vector.tensor_copy(g2[t][:], u[t][:].indirect(n2_t[:]))
+        def smaller(k):
+            mn = u[PACK - 1][:, S:].bitcast(BF16).rearrange("p (e j) -> p e j", e=2) if k == 0 else mn_last[:]
+            nc.vector.tensor_tensor(mn, mx[k][:], g2[k][:], ALU.min)
+            for e in range(2):
+                t = 2 * k + e
+                nc.scalar.activation(zs[:, t, :], mn[:, e, :], ACT.Copy, scale=sign[:, t : t + 1])
 
-        def larger(t):
-            mx[t] = arena.tile([P, S], BF16, name=f"mx_{t}", offset=place["mx", t])
-            nc.vector.tensor_tensor(mx[t][:], ub[t][:], g1[t][:], ALU.max)
-
-        def smaller(t):
-            mn = u[t + 1][:, S:].bitcast(BF16)[:, :S] if t + 1 < PACK else mn_last[:]
-            nc.vector.tensor_tensor(mn, mx[t][:], g2[t][:], ALU.min)
-            nc.scalar.activation(zs[:, t, :], mn, ACT.Copy, scale=sign[:, t : t + 1])
-
-        for t in range(PACK):
-            if t + 1 < PACK:
-                first_product(t + 1, 0, S)
-            pick1(t)
-            pick2(t)
-            larger(t)
-            nc.scalar.copy(y[t][:, :S], y_ps[t][:])
-            if t > 0:
-                smaller(t - 1)
+        for k in range(2):
+            g1[k] = arena.tile([P, 2, S], BF16, name=f"g1_{k}", offset=place["g1", k])
+            g2[k] = arena.tile([P, 2, S], BF16, name=f"g2_{k}", offset=place["g2", k])
+            for e in range(2):
+                t = 2 * k + e
+                nc.vector.tensor_copy(g1[k][:, e, :], u[t][:].indirect(n1_t[:]))
+                nc.vector.tensor_copy(g2[k][:, e, :], u[t][:].indirect(n2_t[:]))
+            larger(k)
+        smaller(0)
 
         w2s = arena.tile([P, N], U8, name="w2s", align_bytes=64, offset=place["g1", 0])
         deal(w2s[:], w2s_raw[:], 16)
         d, g4, th, o, h_ps = {}, {}, {}, {}, {}
         d[0] = arena.tile([P, PACK, 256], F32, name="d0", offset=place["zs"] + 0)
         d_late = arena.tile([P, PACK - 1, 256], F32, name="d_late", offset=place["d0"])
-        d_first = arena.tile([P, 256], F32, name="d_first", offset=place["mx", 3])
+        d_first = arena.tile([P, 256], F32, name="d_first", offset=place["mx", 1])
         for c, (a, w) in enumerate(CHUNKS):
-            th[c] = keep.tile([P, PACK, w], F32, name=f"th{c}")
+            th[c] = arena.tile([P, PACK, w], F32, name=f"th{c}", offset=(30 - 4 * c) * KB)
             o[c] = keep.tile([P, PACK, w], F32, name=f"o{c}")
 
         def pick4(t):
@@ -200,7 +204,7 @@ def tile_picked_skipjointbminmx_none_po_kernel(
             a, w = CHUNKS[c]
             per_bank = S // w
             for b in range(PACK // per_bank):
-                h_ps[c, b] = psum.tile([P, per_bank, w], F32, name=f"h_ps{c}_{b}")
+                h_ps[c, b] = psum.tile([P, per_bank, w], F32, name=f"h_ps{c}_{b}", tag=f"h_ps{c}_{b}")
                 for i in range(per_bank):
                     t = b * per_bank + i
                     m = slice(t * P, (t + 1) * P)
@@ -209,7 +213,10 @@ def tile_picked_skipjointbminmx_none_po_kernel(
                         rhs=zq[:, a : a + w].bitcast(FP8X4), rhs_scale=zqs[:, a : a + w], start=True, stop=True,
                     )
 
-        oq = keep.tile([P, S], U32, name="oq", align_bytes=64)
+        oq = [
+            arena.tile([P, w], U32, name=f"oq{c}", align_bytes=64, offset=place["d0"] if c == 0 else 24 * KB)
+            for c, (a, w) in enumerate(CHUNKS)
+        ]
         oqs = keep.tile([P, S], U8, name="oqs", align_bytes=64)
         oi = {}
         out_rows = out_0.rearrange("(p t) j -> p t j", t=PACK)
@@ -223,9 +230,13 @@ def tile_picked_skipjointbminmx_none_po_kernel(
                 o[c][:, t0:t1, :], h_ps[c, b][:, t0 - b * per_bank : t1 - b * per_bank, :], th[c][:, t0:t1, :], ALU.mult
             )
 
+        def gate_and_store(c, t0, t1):
+            a, w = CHUNKS[c]
+            gate(c, t0, t1)
+            nc.sync.dma_start(out=out_rows[:, t0:t1, a : a + w], in_=o[c][:, t0:t1, :])
+
         def weave_out(c, engines):
             a, w = CHUNKS[c]
-            nc.sync.dma_start(out=out_rows[:, :, a : a + w], in_=o[c][:])
             oi[c] = keep.tile([P, w, PACK], BF16, name=f"oi{c}", align_bytes=64)
             share = w // len(engines)
             for k, copy in enumerate(engines):
@@ -234,16 +245,19 @@ def tile_picked_skipjointbminmx_none_po_kernel(
                     o[c][:, :, k * share : (k + 1) * share].rearrange("p t (c i) -> p c t i", i=4),
                 )
 
-        def quantize_out(c):
+        def quantize_out(c, pieces):
             a, w = CHUNKS[c]
-            nc.vector.quantize_mx(
-                out=oq[:, a : a + w].bitcast(FP8X4), scales=oqs[:, a : a + w],
-                in_=oi[c][:].rearrange("p c t -> p (c t)"),
-            )
-            nc.sync.dma_start(out=out_words[:, a : a + w], in_=oq[:, a : a + w].bitcast(I32))
+            share = w // pieces
+            for k in range(pieces):
+                cols = slice(k * share, (k + 1) * share)
+                nc.vector.quantize_mx(
+                    out=oq[c][:, cols].bitcast(FP8X4), scales=oqs[:, a + k * share : a + (k + 1) * share],
+                    in_=oi[c][:, cols, :].rearrange("p c t -> p (c t)"),
+                )
+            nc.sync.dma_start(out=out_words[:, a : a + w], in_=oq[c][:].bitcast(I32))
 
         pick4(0)
-        smaller(PACK - 1)
+        smaller(1)
         weave_z()
         for t in range(1, PACK):
             pick4(t)
@@ -253,16 +267,16 @@ def tile_picked_skipjointbminmx_none_po_kernel(
         for t in range(PACK):
             pick3(0, t)
         pick3(1, 0)
-        gate(0, 0, 2)
-        gate(0, 2, 4)
+        gate_and_store(0, 0, 2)
+        gate_and_store(0, 2, 4)
         weave_out(0, [nc.scalar.copy])
         for t in range(1, PACK):
             pick3(1, t)
-        quantize_out(0)
-        gate(1, 0, 2)
-        gate(1, 2, 4)
+        gate_and_store(1, 0, 2)
+        gate_and_store(1, 2, 4)
+        quantize_out(0, 1)
         weave_out(1, [nc.scalar.copy, nc.vector.tensor_copy])
-        quantize_out(1)
+        quantize_out(1, 2)
 
         scale_rows = out_2[0].bitcast(I32)
         live = oqs[:].bitcast(I32)

from contextlib import ExitStack

import concourse.mybir as mybir

K, T, S, N, H = 512, 2048, 512, 512, 512
FLOPS = 2 * K * H * S + 2 * H * N * S

F32 = mybir.dt.float32
BF16 = mybir.dt.bfloat16
I32 = mybir.dt.int32
U32 = mybir.dt.uint32
U16 = mybir.dt.uint16
U8 = mybir.dt.uint8
FP8X4 = mybir.dt.float8_e4m3fn_x4
ALU = mybir.AluOpType
ACT = mybir.ActivationFunctionType

P = 128
PACK = 4
W1_ROW = 4
W2_ROW = 8
CHUNKS = ((0, 256), (256, 256))


def load_scale_rows(queue, tile, first_row, scales, which=range(4)):
    rows = scales[0].bitcast(I32)
    view = tile[:].bitcast(I32)
    for r in which:
        queue.dma_start(out=view[first_row + r : P : 32, :], in_=rows[r:16:4, :])


def tile_picked_skipjointbminmx_none_po_kernel(
    tc, x_words, x_scales, w1_words, w1_scales, gn, w2_words, w2_scales, offs, n1, n2, n3, n4, out_0, out_1, out_2
):
    nc = tc.nc
    with ExitStack() as ctx:
        lists = ctx.enter_context(tc.tile_pool(name="lists", bufs=1))
        keep = ctx.enter_context(tc.tile_pool(name="keep", bufs=1))
        arena = ctx.enter_context(tc.tile_pool(name="arena", bufs=1))
        head = ctx.enter_context(tc.tile_pool(name="head", bufs=1))
        psum = ctx.enter_context(tc.psum_pool(name="psum", bufs=1))

        def words_of(dram):
            return dram[0].rearrange("p n t -> p (n t)").bitcast(I32)

        offs_t = lists.tile([P, S // 16], U16, name="offs_t")
        n1_t = lists.tile([P, S // 16], U16, name="n1_t")
        n2_t = lists.tile([P, S // 16], U16, name="n2_t")
        n3_t = lists.tile([P, S // 16], U16, name="n3_t")
        n4_t = lists.tile([P, S // 16], U16, name="n4_t")

        xw = head.tile([P, T], I32, name="xw", align_bytes=64, offset=0)
        xs = keep.tile([P, T], U8, name="xs", align_bytes=64)
        w1_raw = keep.tile([P, H], I32, name="w1_raw", align_bytes=64)
        w2_raw = keep.tile([P, N], I32, name="w2_raw", align_bytes=64)
        w1s_raw = keep.tile([P, H], U8, name="w1s_raw", align_bytes=64)
        w2s_raw = keep.tile([P, N], U8, name="w2s_raw", align_bytes=64)
        gn_t = keep.tile([P, PACK], F32, name="gn_t")

        nc.gpsimd.memset(xs[:].bitcast(I32), 0)
        nc.gpsimd.memset(w1s_raw[:].bitcast(I32), 0)
        nc.gpsimd.memset(w2s_raw[:].bitcast(I32), 0)

        nc.sync.dma_start(offs_t[:], offs)
        nc.sync.dma_start(n1_t[:], n1)
        load_scale_rows(nc.sync, xs, 0, x_scales)
        nc.sync.dma_start(out=xw[:], in_=words_of(x_words))
        nc.sync.dma_start(out=w1_raw[:], in_=words_of(w1_words))
        nc.gpsimd.dma_start(out=gn_t[:], in_=gn.rearrange("(p t) o -> p (t o)", t=PACK))
        load_scale_rows(nc.sync, w1s_raw, W1_ROW, w1_scales)
        nc.sync.dma_start(out=w2_raw[:], in_=words_of(w2_words))
        nc.sync.dma_start(n2_t[:], n2)
        nc.sync.dma_start(n4_t[:], n4)
        load_scale_rows(nc.sync, w2s_raw, W2_ROW, w2_scales)
        nc.sync.dma_start(n3_t[:], n3)

        twice = keep.tile([P, PACK], F32, name="twice")
        sign = keep.tile([P, PACK], F32, name="sign_t")
        mag = keep.tile([P, PACK], F32, name="mag")
        nc.gpsimd.tensor_scalar(twice[:], gn_t[:], 0.0, 2.0, ALU.is_ge, ALU.mult)
        nc.gpsimd.tensor_scalar(sign[:], twice[:], 1.0, -1.0, ALU.mult, ALU.add)
        nc.gpsimd.tensor_tensor(mag[:], gn_t[:], sign[:], ALU.mult)
        warm = keep.tile([P, 1], F32, name="warm")
        nc.scalar.activation(warm[:], gn_t[:, 0:1], ACT.Tanh)

        u = [keep.tile([P, 2 * S], F32, name=f"u{t}") for t in range(PACK)]
        y = [keep.tile([P, 2 * S], F32, name=f"y{t}") for t in range(PACK)]
        ub = [keep.tile([P, 2, S], BF16, name=f"ub{k}") for k in range(2)]

        xg = keep.tile([P, S], U32, name="xg", align_bytes=64)
        xsg = keep.tile([P, S], U8, name="xsg", align_bytes=64)
        w1 = head.tile([P, H], U32, name="w1", align_bytes=64, offset=0)
        w2 = head.tile([P, N], U32, name="w2", align_bytes=64, offset=2048)
        w1s = head.tile([P, H], U8, name="w1s", align_bytes=64, offset=4096)

        def deal(dst, src, line, t0=0, t1=PACK):
            nc.vector.tensor_copy(
                dst.rearrange("p (t c i) -> p c t i", t=PACK, i=line)[:, :, t0:t1, :],
                src.rearrange("p (c i t) -> p c t i", t=PACK, i=line)[:, :, t0:t1, :],
            )

        nc.vector.tensor_copy(xsg[:], xs[:].indirect(offs_t[:]))
        nc.vector.tensor_copy(xg[:], xw[:].bitcast(U32).indirect(offs_t[:]))
        deal(w1[:], w1_raw[:].bitcast(U32), 4, 0, 1)
        deal(w1s[:], w1s_raw[:], 16, 0, 1)
        deal(w1[:], w1_raw[:].bitcast(U32), 4, 1, PACK)
        deal(w1s[:], w1s_raw[:], 16, 1, PACK)
        deal(w2[:], w2_raw[:].bitcast(U32), 4)

        y_ps = [psum.tile([P, S], F32, name=f"y_ps{t}") for t in range(PACK)]
        half = S // 2
        y_late = psum.tile([P, half], F32, name="y_late", tag="h_ps1_1")

        def first_product(t, bank, a, b):
            m = slice(t * P, (t + 1) * P)
            nc.tensor.matmul_mx(
                out=bank, lhsT=w1[:, m].bitcast(FP8X4), lhsT_scale=w1s[W1_ROW:P, m],
                rhs=xg[:, a:b].bitcast(FP8X4), rhs_scale=xsg[:, a:b], start=True, stop=True,
            )

        def scaled(dst, bank, t):
            nc.scalar.activation(dst, bank, ACT.Copy, scale=mag[:, t : t + 1])

        first_product(0, y_ps[0][:, :half], 0, half)
        first_product(0, y_late[:], half, S)
        scaled(u[0][:, :half], y_ps[0][:, :half], 0)
        nc.vector.tensor_scalar(u[0][:, half:S], y_late[:], mag[:, 0:1], None, ALU.mult)
        nc.scalar.copy(ub[0][:, 0, :], u[0][:, :S])
        for t in range(1, PACK):
            first_product(t, y_ps[t][:], 0, S)
            scaled(ub[t // 2][:, t % 2, :], y_ps[t][:], t)
            scaled(u[t][:, :S], y_ps[t][:], t)
        nc.scalar.copy(y[0][:, :half], y_ps[0][:, :half])
        nc.scalar.copy(y[0][:, half:S], y_late[:])
        for t in range(1, PACK):
            nc.scalar.copy(y[t][:, :S], y_ps[t][:])

        KB = 1024
        place = {"zs": 0, "d0": 0, ("g1", 0): 4 * KB, ("g2", 0): 6 * KB, ("mx", 0): 8 * KB, ("mx", 1): 10 * KB}
        place["g1", 1] = 14 * KB
        place["g2", 1] = 20 * KB
        g4_place = [place["g1", 1] - KB, place["g1", 1] + KB, place["g2", 1] - KB, place["g2", 1] + KB]
        zs = arena.tile([P, PACK, S], BF16, name="zs", offset=place["zs"])
        g1, g2, mx = {}, {}, {}
        mn_last = arena.tile([P, 2, S], BF16, name="mn_last", offset=26 * KB)

        def larger(k):
            mx[k] = arena.tile([P, 2, S], BF16, name=f"mx_{k}", offset=place["mx", k])
            nc.vector.tensor_tensor(mx[k][:], ub[k][:], g1[k][:], ALU.max)

        def smaller(k):
            mn = u[PACK - 1][:, S:].bitcast(BF16).rearrange("p (e j) -> p e j", e=2) if k == 0 else mn_last[:]
            nc.vector.tensor_tensor(mn, mx[k][:], g2[k][:], ALU.min)
            for e in range(2):
                t = 2 * k + e
                nc.scalar.activation(zs[:, t, :], mn[:, e, :], ACT.Copy, scale=sign[:, t : t + 1])

        for k in range(2):
            g1[k] = arena.tile([P, 2, S], BF16, name=f"g1_{k}", offset=place["g1", k])
            g2[k] = arena.tile([P, 2, S], BF16, name=f"g2_{k}", offset=place["g2", k])
            for e in range(2):
                t = 2 * k + e
                nc.vector.tensor_copy(g1[k][:, e, :], u[t][:].indirect(n1_t[:]))
                nc.vector.tensor_copy(g2[k][:, e, :], u[t][:].indirect(n2_t[:]))
            larger(k)
        smaller(0)

        w2s = arena.tile([P, N], U8, name="w2s", align_bytes=64, offset=place["g1", 0])
        deal(w2s[:], w2s_raw[:], 16)
        d, g4, th, o, h_ps = {}, {}, {}, {}, {}
        d[0] = arena.tile([P, PACK, 256], F32, name="d0", offset=place["zs"] + 0)
        d_late = arena.tile([P, PACK - 1, 256], F32, name="d_late", offset=place["d0"])
        d_first = arena.tile([P, 256], F32, name="d_first", offset=place["mx", 1])
        for c, (a, w) in enumerate(CHUNKS):
            th[c] = arena.tile([P, PACK, w], F32, name=f"th{c}", offset=(30 - 4 * c) * KB)
            o[c] = keep.tile([P, PACK, w], F32, name=f"o{c}")

        def pick4(t):
            g4[t] = arena.tile([P, S], F32, name=f"g4_{t}", offset=g4_place[t])
            nc.vector.tensor_copy(g4[t][:], y[t][:].indirect(n4_t[:]))

        def pick3(c, t):
            a, w = CHUNKS[c]
            diff = d[0][:, t, :] if c == 0 else (d_first[:] if t == 0 else d_late[:, t - 1, :])
            nc.vector.tensor_tensor(
                diff, y[t][:].indirect(n3_t[:, a // 16 : (a + w) // 16]), g4[t][:, a : a + w], ALU.subtract
            )
            nc.scalar.activation(th[c][:, t, :], diff, ACT.Tanh)

        zq = keep.tile([P, S], U32, name="zq", align_bytes=64)
        zqs = keep.tile([P, S], U8, name="zqs", align_bytes=64)
        zi = keep.tile([P, S, PACK], BF16, name="zi", align_bytes=64)

        def weave_z():
            nc.scalar.copy(
                zi[:].rearrange("p (c i) t -> p c t i", i=4),
                zs[:].rearrange("p t (c i) -> p c t i", i=4),
            )

        def quantize_z():
            nc.vector.quantize_mx(out=zq[:].bitcast(FP8X4), scales=zqs[:], in_=zi[:].rearrange("p c t -> p (c t)"))

        def second_product(c):
            a, w = CHUNKS[c]
            per_bank = S // w
            for b in range(PACK // per_bank):
                h_ps[c, b] = psum.tile([P, per_bank, w], F32, name=f"h_ps{c}_{b}", tag=f"h_ps{c}_{b}")
                for i in range(per_bank):
                    t = b * per_bank + i
                    m = slice(t * P, (t + 1) * P)
                    nc.tensor.matmul_mx(
                        out=h_ps[c, b][:, i, :], lhsT=w2[:, m].bitcast(FP8X4), lhsT_scale=w2s[W2_ROW:P, m],
                        rhs=zq[:, a : a + w].bitcast(FP8X4), rhs_scale=zqs[:, a : a + w], start=True, stop=True,
                    )

        oq = [
            arena.tile([P, w], U32, name=f"oq{c}", align_bytes=64, offset=place["d0"] if c == 0 else 24 * KB)
            for c, (a, w) in enumerate(CHUNKS)
        ]
        oqs = keep.tile([P, S], U8, name="oqs", align_bytes=64)
        oi = {}
        out_rows = out_0.rearrange("(p t) j -> p t j", t=PACK)
        out_words = words_of(out_1)

        def gate(c, t0, t1):
            a, w = CHUNKS[c]
            per_bank = S // w
            b = t0 // per_bank
            nc.vector.tensor_tensor(
                o[c][:, t0:t1, :], h_ps[c, b][:, t0 - b * per_bank : t1 - b * per_bank, :], th[c][:, t0:t1, :], ALU.mult
            )

        def gate_and_store(c, t0, t1):
            a, w = CHUNKS[c]
            gate(c, t0, t1)
            nc.sync.dma_start(out=out_rows[:, t0:t1, a : a + w], in_=o[c][:, t0:t1, :])

        def weave_out(c, engines):
            a, w = CHUNKS[c]
            oi[c] = keep.tile([P, w, PACK], BF16, name=f"oi{c}", align_bytes=64)
            share = w // len(engines)
            for k, copy in enumerate(engines):
                copy(
                    oi[c][:, k * share : (k + 1) * share, :].rearrange("p (c i) t -> p c t i", i=4),
                    o[c][:, :, k * share : (k + 1) * share].rearrange("p t (c i) -> p c t i", i=4),
                )

        def quantize_out(c, pieces):
            a, w = CHUNKS[c]
            share = w // pieces
            for k in range(pieces):
                cols = slice(k * share, (k + 1) * share)
                nc.vector.quantize_mx(
                    out=oq[c][:, cols].bitcast(FP8X4), scales=oqs[:, a + k * share : a + (k + 1) * share],
                    in_=oi[c][:, cols, :].rearrange("p c t -> p (c t)"),
                )
            nc.sync.dma_start(out=out_words[:, a : a + w], in_=oq[c][:].bitcast(I32))

        pick4(0)
        smaller(1)
        weave_z()
        for t in range(1, PACK):
            pick4(t)
        quantize_z()
        second_product(0)
        second_product(1)
        for t in range(PACK):
            pick3(0, t)
        pick3(1, 0)
        gate_and_store(0, 0, 2)
        gate_and_store(0, 2, 4)
        weave_out(0, [nc.scalar.copy])
        for t in range(1, PACK):
            pick3(1, t)
        gate_and_store(1, 0, 2)
        gate_and_store(1, 2, 4)
        quantize_out(0, 1)
        weave_out(1, [nc.scalar.copy, nc.vector.tensor_copy])
        quantize_out(1, 2)

        scale_rows = out_2[0].bitcast(I32)
        live = oqs[:].bitcast(I32)
        for q in range(4):
            queue = nc.sync if q % 2 == 0 else nc.scalar
            queue.dma_start(out=scale_rows[4 * q : 4 * q + 4, :], in_=live[32 * q : 32 * q + 4, :])
